import numpy as np
CORES = [0,1,2,3,4,5,6,7,128,129,130,131,132,133,134,135,256,257,258,259,260,261,262,263,384,385,386,387,388,389,390,391]
N = 32
WIDTHS = [0,4,4,0,0,0,2,2,8,1,1,8,0,8,1,2,0,8,0,2,4,16,2,2,0,4,4,1,1,4,2,1]
OFF = [0,0,4,8,8,8,8,10,12,20,21,22,30,30,38,39,41,41,49,49,51,55,71,73,75,75,79,83,84,85,89,91]
C = 92
def setup_inputs(rng):
    return {"x": rng.standard_normal((N, 128, C), dtype=np.float32)}
def reference(x):
    s = x.sum(axis=0, dtype=np.float64).astype(x.dtype)
    YW = max(WIDTHS)
    y = np.full((N, 128, YW), np.nan, x.dtype)
    for r in range(N):
        y[r][:, :WIDTHS[r]] = s[:, OFF[r]:OFF[r] + WIDTHS[r]]
    return {"y": y}

@@ -1,0 +1,128 @@
+from concourse.bass import DstId, RemoteDMATransfer
+from concourse.mybir import AluOpType
+
+AGENTS = [
+    [(0, 0, 92)],
+    [(4, 0, 92)],
+    [(0, 0, 92)],
+    [(0, 0, 92)],
+]
+RW = max(sum(b - a for k, a, b in host if k == c) for host in AGENTS for c in range(8))
+
+SCRATCH = {
+    "xs": ("sbuf", [128, 92], "float32"),
+    "land1": ("sbuf", [128, 7, RW], "float32"),
+    "land2": ("sbuf", [128, RW], "float32"),
+    "land3": ("sbuf", [128, 32], "float32"),
+}
+SEMAPHORES = ["loc", "a1", "a2", "a3", "sent"]
+
+PLANS = {}
+
+
+def runs(items):
+    out = []
+    for it in items:
+        if out:
+            first, n = out[-1]
+            if it[0] == first[0] and all(it[i] == first[i] + n for i in range(1, len(it))):
+                out[-1] = (first, n + 1)
+                continue
+        out.append((it, 1))
+    return out
+
+
+def make_plan(W, OFF, C):
+    owner = [None] * C
+    for r in range(len(W)):
+        for c in range(OFF[r], OFF[r] + W[r]):
+            owner[c] = r
+    ag = [[None] * C for _ in range(4)]
+    loc = [[None] * C for _ in range(4)]
+    for H in range(4):
+        used = [0] * 8
+        for k, a, b in AGENTS[H]:
+            for c in range(a, b):
+                ag[H][c], loc[H][c] = k, used[k]
+                used[k] += 1
+    sends = []
+    for H in range(4):
+        for k, a, b in AGENTS[H]:
+            for c in range(8):
+                if c != k:
+                    sends.append((1, H, c, H, k, a, b - a, a, loc[H][a]))
+        for k in range(8):
+            mine = [c for c in range(C) if ag[H][c] == k]
+            D = H ^ 1
+            s2 = [((ag[D][c],), c, loc[H][c], loc[D][c]) for c in mine if owner[c] // 8 in (H ^ 1, H ^ 2)]
+            for (key, c, lo, dlo), n in runs(s2):
+                sends.append((2, H, k, D, key[0], c, n, lo, dlo))
+            for g in (3 - H, H):
+                s3 = [((owner[c],), c, loc[H][c]) for c in mine if owner[c] // 8 == g]
+                for (key, c, lo), n in runs(s3):
+                    r = key[0]
+                    assert (g, r % 8) != (H, k), "an agent may not fold into itself"
+                    sends.append((3, H, k, g, r % 8, c, n, lo, c - OFF[r] + (0 if g == H else W[r])))
+    return sends
+
+
+def rank_program(g, core, T, topo):
+    rank = T.rank_of(core)
+    if rank is None:
+        return
+    W, OFF, C = T.tables["WIDTHS"], T.tables["OFF"], T.tables["C"]
+    if "p" not in PLANS:
+        PLANS["p"] = make_plan(W, OFF, C)
+    sends = PLANS["p"]
+    H, k = rank // 8, rank % 8
+    world = lambda h, c: T.cores[8 * h + c]
+    engines = lambda m: bin(m).count("1")
+
+    due = {1: 0, 2: 0, 3: 0}
+    sent = 0
+    for s in sends:
+        m = engines(topo.mask(world(s[1], s[2]), world(s[3], s[4])))
+        if (s[3], s[4]) == (H, k):
+            due[s[0]] += m
+        if (s[1], s[2]) == (H, k):
+            sent += m
+    mine = [s for s in sends if (s[1], s[2]) == (H, k)]
+    arr = {1: T.sem.a1, 2: T.sem.a2, 3: T.sem.a3}
+
+    g.dma_start(T.xs[:], T.x[:]).then_inc(T.sem.loc, 16)
+    g.wait_ge(T.sem.loc, 16)
+
+    for _, _, _, dh, dc, col, n, _, dlo in [s for s in mine if s[0] == 1]:
+        dst = world(dh, dc)
+        rid, pid = topo.addr(dst, core)
+        slot = k if k < dc else k - 1
+        g.remote_dma(T.land1[:, slot, dlo:dlo + n], T.xs[:, col:col + n], T.sem.a1, T.sem.sent, pid, rid,
+                     topo.mask(core, dst))
+
+    for step in (2, 3):
+        todo = [s for s in mine if s[0] == step]
+        if not todo:
+            continue
+        g.wait_ge(arr[step - 1], due[step - 1])
+        for _, _, _, dh, dc, col, n, lo, dlo in todo:
+            dst = world(dh, dc)
+            rid, pid = topo.addr(dst, core)
+            srcs = [T.xs[:, col:col + n]] + [T.land1[:, s, lo:lo + n] for s in range(7)]
+            if step == 3:
+                srcs.append(T.land2[:, lo:lo + n])
+            out = T.land2[:, dlo:dlo + n] if step == 2 else T.land3[:, dlo:dlo + n]
+            g.remote_dma_fused([RemoteDMATransfer(dst_ids=[DstId(rid=rid, pnc=pid)], dma_engine_mask=topo.mask(core, dst),
+                                                  remote_sem=arr[step], srcs=srcs, dsts=[out], alu_op=1)],
+                               local_sem=T.sem.sent)
+    for step in (1, 2):
+        if due[step] and not [s for s in mine if s[0] == step + 1]:
+            g.wait_ge(arr[step], due[step])
+
+    w = W[rank]
+    if w:
+        g.wait_ge(T.sem.a3, due[3])
+        g.dma_start(T.land3[:, 0:w], T.land3[:, w:2 * w], accum_op=AluOpType.add).then_inc(T.sem.loc, 16)
+        g.wait_ge(T.sem.loc, 32)
+        g.dma_start(T.y[:, 0:w], T.land3[:, 0:w], allow_slow_non_contiguous=(w == 1)).then_inc(T.sem.loc, 16)
+        g.wait_ge(T.sem.loc, 48)
+    g.wait_ge(T.sem.sent, sent)

@@ -2,10 +2,10 @@ from concourse.bass import DstId, RemoteDMATransfer
 from concourse.mybir import AluOpType
 
 AGENTS = [
-    [(0, 0, 92)],
-    [(4, 0, 92)],
-    [(0, 0, 92)],
-    [(0, 0, 92)],
+    [(5, 0, 25), (4, 25, 43), (2, 43, 66), (1, 66, 84), (3, 84, 92)],
+    [(6, 0, 25), (1, 25, 48), (7, 48, 57), (3, 57, 66), (4, 66, 92)],
+    [(2, 0, 21), (5, 21, 30), (1, 30, 39), (7, 39, 55), (6, 55, 71), (3, 71, 92)],
+    [(6, 0, 4), (5, 4, 21), (1, 21, 42), (4, 42, 64), (0, 64, 84), (3, 84, 92)],
 ]
 RW = max(sum(b - a for k, a, b in host if k == c) for host in AGENTS for c in range(8))
 
@@ -14,6 +14,11 @@ SCRATCH = {
     "land1": ("sbuf", [128, 7, RW], "float32"),
     "land2": ("sbuf", [128, RW], "float32"),
     "land3": ("sbuf", [128, 32], "float32"),
+    "pq1": ("dram", [2, 128, 1], "float32"),
+    "pq2": ("dram", [2, 128, 2], "float32"),
+    "pq4": ("dram", [2, 128, 4], "float32"),
+    "pq8": ("dram", [2, 128, 8], "float32"),
+    "pq16": ("dram", [2, 128, 16], "float32"),
 }
 SEMAPHORES = ["loc", "a1", "a2", "a3", "sent"]
 
@@ -32,7 +37,14 @@ def runs(items):
     return out
 
 
-def make_plan(W, OFF, C):
+def pow2_at_least(n):
+    p = 1
+    while p < n:
+        p *= 2
+    return p
+
+
+def make_plan(W, OFF, C, agents):
     owner = [None] * C
     for r in range(len(W)):
         for c in range(OFF[r], OFF[r] + W[r]):
@@ -41,29 +53,64 @@ def make_plan(W, OFF, C):
     loc = [[None] * C for _ in range(4)]
     for H in range(4):
         used = [0] * 8
-        for k, a, b in AGENTS[H]:
+        for k, a, b in agents[H]:
             for c in range(a, b):
+                assert ag[H][c] is None
                 ag[H][c], loc[H][c] = k, used[k]
                 used[k] += 1
     sends = []
+
+    def add(step, H, k, dh, dc, col, n, lo, where, dlo):
+        sends.append({"step": step, "src": (H, k), "dst": (dh, dc), "col": col, "n": n, "lo": lo, "where": where, "dlo": dlo})
+
     for H in range(4):
-        for k, a, b in AGENTS[H]:
+        for k, a, b in agents[H]:
             for c in range(8):
                 if c != k:
-                    sends.append((1, H, c, H, k, a, b - a, a, loc[H][a]))
+                    add(1, H, c, H, k, a, b - a, a, "land1", loc[H][a])
         for k in range(8):
             mine = [c for c in range(C) if ag[H][c] == k]
             D = H ^ 1
             s2 = [((ag[D][c],), c, loc[H][c], loc[D][c]) for c in mine if owner[c] // 8 in (H ^ 1, H ^ 2)]
-            for (key, c, lo, dlo), n in runs(s2):
-                sends.append((2, H, k, D, key[0], c, n, lo, dlo))
+            pieces = runs(s2)
+            pieces.sort(key=lambda p: 0 if any(owner[c] // 8 == H ^ 2 for c in range(p[0][1], p[0][1] + p[1])) else 1)
+            for (key, c, lo, dlo), n in pieces:
+                add(2, H, k, D, key[0], c, n, lo, "land2", dlo)
             for g in (3 - H, H):
                 s3 = [((owner[c],), c, loc[H][c]) for c in mine if owner[c] // 8 == g]
                 for (key, c, lo), n in runs(s3):
                     r = key[0]
-                    assert (g, r % 8) != (H, k), "an agent may not fold into itself"
-                    sends.append((3, H, k, g, r % 8, c, n, lo, c - OFF[r] + (0 if g == H else W[r])))
-    return sends
+                    assert (g, r % 8) != (H, k), "a fold may not name its own core"
+                    add(3, H, k, g, r % 8, c, n, lo, "land3", c - OFF[r] + (0 if g == H else W[r]))
+    whole = set()
+    for r in range(len(W)):
+        got = [s for s in sends if s["step"] == 3 and s["dst"] == (r // 8, r % 8)]
+        if W[r] and len(got) == 2:
+            whole.add(r)
+            for s in got:
+                s["where"], s["dlo"] = "pq", (0 if s["src"][0] == r // 8 else 1)
+    for H in range(4):
+        for k in range(8):
+            call = 0
+            for step in (1, 2, 3):
+                todo = [s for s in sends if s["src"] == (H, k) and s["step"] == step]
+                leaves = any(s["dst"][0] != H for s in todo)
+                widths = []
+                for s in todo:
+                    if s["n"] not in widths:
+                        widths.append(s["n"])
+                for n in widths:
+                    grp = [s for s in todo if s["n"] == n]
+                    for pool, base, size in (([s for s in grp if s["dst"][0] != H], 0, 8),
+                                             ([s for s in grp if s["dst"][0] == H], 8 if leaves else 0, 8 if leaves else 16)):
+                        if pool:
+                            e = size // pow2_at_least(len(pool))
+                            assert e >= 1
+                            for i, s in enumerate(pool):
+                                s["mask"] = ((1 << e) - 1) << (base + i * e)
+                                s["call"] = call
+                    call += 1
+    return sends, whole
 
 
 def rank_program(g, core, T, topo):
@@ -72,57 +119,66 @@ def rank_program(g, core, T, topo):
         return
     W, OFF, C = T.tables["WIDTHS"], T.tables["OFF"], T.tables["C"]
     if "p" not in PLANS:
-        PLANS["p"] = make_plan(W, OFF, C)
-    sends = PLANS["p"]
-    H, k = rank // 8, rank % 8
-    world = lambda h, c: T.cores[8 * h + c]
+        PLANS["p"] = make_plan(W, OFF, C, AGENTS)
+    sends, whole = PLANS["p"]
+    me = (rank // 8, rank % 8)
+    k = me[1]
     engines = lambda m: bin(m).count("1")
 
     due = {1: 0, 2: 0, 3: 0}
-    sent = 0
     for s in sends:
-        m = engines(topo.mask(world(s[1], s[2]), world(s[3], s[4])))
-        if (s[3], s[4]) == (H, k):
-            due[s[0]] += m
-        if (s[1], s[2]) == (H, k):
-            sent += m
-    mine = [s for s in sends if (s[1], s[2]) == (H, k)]
+        if s["dst"] == me:
+            due[s["step"]] += engines(s["mask"])
+    mine = [s for s in sends if s["src"] == me]
+    sent = sum(engines(s["mask"]) for s in mine)
     arr = {1: T.sem.a1, 2: T.sem.a2, 3: T.sem.a3}
+    waited = []
+
+    def need(step):
+        if due[step] and step not in waited:
+            g.wait_ge(arr[step], due[step])
+            waited.append(step)
 
     g.dma_start(T.xs[:], T.x[:]).then_inc(T.sem.loc, 16)
     g.wait_ge(T.sem.loc, 16)
 
-    for _, _, _, dh, dc, col, n, _, dlo in [s for s in mine if s[0] == 1]:
-        dst = world(dh, dc)
-        rid, pid = topo.addr(dst, core)
-        slot = k if k < dc else k - 1
-        g.remote_dma(T.land1[:, slot, dlo:dlo + n], T.xs[:, col:col + n], T.sem.a1, T.sem.sent, pid, rid,
-                     topo.mask(core, dst))
-
-    for step in (2, 3):
-        todo = [s for s in mine if s[0] == step]
-        if not todo:
-            continue
-        g.wait_ge(arr[step - 1], due[step - 1])
-        for _, _, _, dh, dc, col, n, lo, dlo in todo:
-            dst = world(dh, dc)
+    ncalls = 1 + max([s["call"] for s in mine])
+    for call in range(ncalls):
+        batch = [s for s in mine if s["call"] == call]
+        step = batch[0]["step"]
+        for earlier in range(1, step):
+            need(earlier)
+        transfers = []
+        for s in batch:
+            col, n, lo, dlo = s["col"], s["n"], s["lo"], s["dlo"]
+            dst = T.cores[8 * s["dst"][0] + s["dst"][1]]
+            assert s["mask"] & ~topo.mask(core, dst) == 0
             rid, pid = topo.addr(dst, core)
-            srcs = [T.xs[:, col:col + n]] + [T.land1[:, s, lo:lo + n] for s in range(7)]
+            srcs = [T.xs[:, col:col + n]]
+            if step >= 2:
+                srcs += [T.land1[:, i, lo:lo + n] for i in range(7)]
             if step == 3:
                 srcs.append(T.land2[:, lo:lo + n])
-            out = T.land2[:, dlo:dlo + n] if step == 2 else T.land3[:, dlo:dlo + n]
-            g.remote_dma_fused([RemoteDMATransfer(dst_ids=[DstId(rid=rid, pnc=pid)], dma_engine_mask=topo.mask(core, dst),
-                                                  remote_sem=arr[step], srcs=srcs, dsts=[out], alu_op=1)],
-                               local_sem=T.sem.sent)
-    for step in (1, 2):
-        if due[step] and not [s for s in mine if s[0] == step + 1]:
-            g.wait_ge(arr[step], due[step])
+            if s["where"] == "land1":
+                out = T.land1[:, k if k < s["dst"][1] else k - 1, dlo:dlo + n]
+            elif s["where"] == "pq":
+                out = T["pq%d" % n][dlo]
+            else:
+                out = T[s["where"]][:, dlo:dlo + n]
+            transfers.append(RemoteDMATransfer(dst_ids=[DstId(rid=rid, pnc=pid)], dma_engine_mask=s["mask"],
+                                               remote_sem=arr[step], srcs=srcs, dsts=[out], alu_op=1 if step >= 2 else 0))
+        g.remote_dma_fused(transfers, local_sem=T.sem.sent)
 
+    for step in (1, 2, 3):
+        need(step)
     w = W[rank]
     if w:
-        g.wait_ge(T.sem.a3, due[3])
-        g.dma_start(T.land3[:, 0:w], T.land3[:, w:2 * w], accum_op=AluOpType.add).then_inc(T.sem.loc, 16)
+        if rank in whole:
+            mine_half, other_half = T["pq%d" % w][0], T["pq%d" % w][1]
+        else:
+            mine_half, other_half = T.land3[:, 0:w], T.land3[:, w:2 * w]
+        g.dma_start(mine_half, other_half, accum_op=AluOpType.add).then_inc(T.sem.loc, 16)
         g.wait_ge(T.sem.loc, 32)
-        g.dma_start(T.y[:, 0:w], T.land3[:, 0:w], allow_slow_non_contiguous=(w == 1)).then_inc(T.sem.loc, 16)
+        g.dma_start(T.y[:, 0:w], mine_half, allow_slow_non_contiguous=(w == 1)).then_inc(T.sem.loc, 16)
         g.wait_ge(T.sem.loc, 48)
     g.wait_ge(T.sem.sent, sent)

@@ -2,10 +2,10 @@ from concourse.bass import DstId, RemoteDMATransfer
 from concourse.mybir import AluOpType
 
 AGENTS = [
-    [(5, 0, 25), (4, 25, 43), (2, 43, 66), (1, 66, 84), (3, 84, 92)],
-    [(6, 0, 25), (1, 25, 48), (7, 48, 57), (3, 57, 66), (4, 66, 92)],
-    [(2, 0, 21), (5, 21, 30), (1, 30, 39), (7, 39, 55), (6, 55, 71), (3, 71, 92)],
-    [(6, 0, 4), (5, 4, 21), (1, 21, 42), (4, 42, 64), (0, 64, 84), (3, 84, 92)],
+    [(4, 0, 22), (0, 22, 44), (7, 44, 66), (3, 66, 84), (1, 84, 92)],
+    [(6, 0, 25), (2, 25, 48), (0, 48, 57), (7, 57, 66), (4, 66, 92)],
+    [(6, 0, 21), (3, 21, 30), (4, 30, 39), (0, 39, 55), (2, 55, 76), (7, 76, 92)],
+    [(2, 0, 8), (7, 8, 24), (4, 24, 44), (3, 44, 64), (0, 64, 84), (1, 84, 92)],
 ]
 RW = max(sum(b - a for k, a, b in host if k == c) for host in AGENTS for c in range(8))
 
@@ -20,7 +20,7 @@ SCRATCH = {
     "pq8": ("dram", [2, 128, 8], "float32"),
     "pq16": ("dram", [2, 128, 16], "float32"),
 }
-SEMAPHORES = ["loc", "a1", "a2", "a3", "sent"]
+SEMAPHORES = ["ld", "loc", "a1", "a2", "a3", "sent"]
 
 PLANS = {}
 
@@ -63,8 +63,12 @@ def make_plan(W, OFF, C, agents):
     def add(step, H, k, dh, dc, col, n, lo, where, dlo):
         sends.append({"step": step, "src": (H, k), "dst": (dh, dc), "col": col, "n": n, "lo": lo, "where": where, "dlo": dlo})
 
+    def hops_ahead(H, a, b):
+        hosts = [owner[c] // 8 for c in range(a, b)]
+        return 0 if H ^ 2 in hosts else 1 if H ^ 1 in hosts else 2
+
     for H in range(4):
-        for k, a, b in agents[H]:
+        for k, a, b in sorted(agents[H], key=lambda r: hops_ahead(H, r[1], r[2])):
             for c in range(8):
                 if c != k:
                     add(1, H, c, H, k, a, b - a, a, "land1", loc[H][a])
@@ -72,9 +76,7 @@ def make_plan(W, OFF, C, agents):
             mine = [c for c in range(C) if ag[H][c] == k]
             D = H ^ 1
             s2 = [((ag[D][c],), c, loc[H][c], loc[D][c]) for c in mine if owner[c] // 8 in (H ^ 1, H ^ 2)]
-            pieces = runs(s2)
-            pieces.sort(key=lambda p: 0 if any(owner[c] // 8 == H ^ 2 for c in range(p[0][1], p[0][1] + p[1])) else 1)
-            for (key, c, lo, dlo), n in pieces:
+            for (key, c, lo, dlo), n in sorted(runs(s2), key=lambda p: hops_ahead(H, p[0][1], p[0][1] + p[1])):
                 add(2, H, k, D, key[0], c, n, lo, "land2", dlo)
             for g in (3 - H, H):
                 s3 = [((owner[c],), c, loc[H][c]) for c in mine if owner[c] // 8 == g]
@@ -139,8 +141,8 @@ def rank_program(g, core, T, topo):
             g.wait_ge(arr[step], due[step])
             waited.append(step)
 
-    g.dma_start(T.xs[:], T.x[:]).then_inc(T.sem.loc, 16)
-    g.wait_ge(T.sem.loc, 16)
+    g.sync.dma_start(T.xs[:], T.x[:]).then_inc(T.sem.ld, 16)
+    g.wait_ge(T.sem.ld, 16)
 
     ncalls = 1 + max([s["call"] for s in mine])
     for call in range(ncalls):
@@ -178,7 +180,7 @@ def rank_program(g, core, T, topo):
         else:
             mine_half, other_half = T.land3[:, 0:w], T.land3[:, w:2 * w]
         g.dma_start(mine_half, other_half, accum_op=AluOpType.add).then_inc(T.sem.loc, 16)
-        g.wait_ge(T.sem.loc, 32)
+        g.wait_ge(T.sem.loc, 16)
         g.dma_start(T.y[:, 0:w], mine_half, allow_slow_non_contiguous=(w == 1)).then_inc(T.sem.loc, 16)
-        g.wait_ge(T.sem.loc, 48)
+        g.wait_ge(T.sem.loc, 32)
     g.wait_ge(T.sem.sent, sent)

from concourse.bass import DstId, RemoteDMATransfer
from concourse.mybir import AluOpType

AGENTS = [
    [(4, 0, 22), (0, 22, 44), (7, 44, 66), (3, 66, 84), (1, 84, 92)],
    [(6, 0, 25), (2, 25, 48), (0, 48, 57), (7, 57, 66), (4, 66, 92)],
    [(6, 0, 21), (3, 21, 30), (4, 30, 39), (0, 39, 55), (2, 55, 76), (7, 76, 92)],
    [(2, 0, 8), (7, 8, 24), (4, 24, 44), (3, 44, 64), (0, 64, 84), (1, 84, 92)],
]
RW = max(sum(b - a for k, a, b in host if k == c) for host in AGENTS for c in range(8))

SCRATCH = {
    "xs": ("sbuf", [128, 92], "float32"),
    "land1": ("sbuf", [128, 7, RW], "float32"),
    "land2": ("sbuf", [128, RW], "float32"),
    "land3": ("sbuf", [128, 32], "float32"),
    "pq1": ("dram", [2, 128, 1], "float32"),
    "pq2": ("dram", [2, 128, 2], "float32"),
    "pq4": ("dram", [2, 128, 4], "float32"),
    "pq8": ("dram", [2, 128, 8], "float32"),
    "pq16": ("dram", [2, 128, 16], "float32"),
}
SEMAPHORES = ["ld", "loc", "a1", "a2", "a3", "sent"]

PLANS = {}


def runs(items):
    out = []
    for it in items:
        if out:
            first, n = out[-1]
            if it[0] == first[0] and all(it[i] == first[i] + n for i in range(1, len(it))):
                out[-1] = (first, n + 1)
                continue
        out.append((it, 1))
    return out


def pow2_at_least(n):
    p = 1
    while p < n:
        p *= 2
    return p


def make_plan(W, OFF, C, agents):
    owner = [None] * C
    for r in range(len(W)):
        for c in range(OFF[r], OFF[r] + W[r]):
            owner[c] = r
    ag = [[None] * C for _ in range(4)]
    loc = [[None] * C for _ in range(4)]
    for H in range(4):
        used = [0] * 8
        for k, a, b in agents[H]:
            for c in range(a, b):
                assert ag[H][c] is None
                ag[H][c], loc[H][c] = k, used[k]
                used[k] += 1
    sends = []

    def add(step, H, k, dh, dc, col, n, lo, where, dlo):
        sends.append({"step": step, "src": (H, k), "dst": (dh, dc), "col": col, "n": n, "lo": lo, "where": where, "dlo": dlo})

    def hops_ahead(H, a, b):
        hosts = [owner[c] // 8 for c in range(a, b)]
        return 0 if H ^ 2 in hosts else 1 if H ^ 1 in hosts else 2

    for H in range(4):
        for k, a, b in sorted(agents[H], key=lambda r: hops_ahead(H, r[1], r[2])):
            for c in range(8):
                if c != k:
                    add(1, H, c, H, k, a, b - a, a, "land1", loc[H][a])
        for k in range(8):
            mine = [c for c in range(C) if ag[H][c] == k]
            D = H ^ 1
            s2 = [((ag[D][c],), c, loc[H][c], loc[D][c]) for c in mine if owner[c] // 8 in (H ^ 1, H ^ 2)]
            for (key, c, lo, dlo), n in sorted(runs(s2), key=lambda p: hops_ahead(H, p[0][1], p[0][1] + p[1])):
                add(2, H, k, D, key[0], c, n, lo, "land2", dlo)
            for g in (3 - H, H):
                s3 = [((owner[c],), c, loc[H][c]) for c in mine if owner[c] // 8 == g]
                for (key, c, lo), n in runs(s3):
                    r = key[0]
                    assert (g, r % 8) != (H, k), "a fold may not name its own core"
                    add(3, H, k, g, r % 8, c, n, lo, "land3", c - OFF[r] + (0 if g == H else W[r]))
    whole = set()
    for r in range(len(W)):
        got = [s for s in sends if s["step"] == 3 and s["dst"] == (r // 8, r % 8)]
        if W[r] and len(got) == 2:
            whole.add(r)
            for s in got:
                s["where"], s["dlo"] = "pq", (0 if s["src"][0] == r // 8 else 1)
    for H in range(4):
        for k in range(8):
            call = 0
            for step in (1, 2, 3):
                todo = [s for s in sends if s["src"] == (H, k) and s["step"] == step]
                leaves = any(s["dst"][0] != H for s in todo)
                widths = []
                for s in todo:
                    if s["n"] not in widths:
                        widths.append(s["n"])
                for n in widths:
                    grp = [s for s in todo if s["n"] == n]
                    for pool, base, size in (([s for s in grp if s["dst"][0] != H], 0, 8),
                                             ([s for s in grp if s["dst"][0] == H], 8 if leaves else 0, 8 if leaves else 16)):
                        if pool:
                            e = size // pow2_at_least(len(pool))
                            assert e >= 1
                            for i, s in enumerate(pool):
                                s["mask"] = ((1 << e) - 1) << (base + i * e)
                                s["call"] = call
                    call += 1
    return sends, whole


def rank_program(g, core, T, topo):
    rank = T.rank_of(core)
    if rank is None:
        return
    W, OFF, C = T.tables["WIDTHS"], T.tables["OFF"], T.tables["C"]
    if "p" not in PLANS:
        PLANS["p"] = make_plan(W, OFF, C, AGENTS)
    sends, whole = PLANS["p"]
    me = (rank // 8, rank % 8)
    k = me[1]
    engines = lambda m: bin(m).count("1")

    due = {1: 0, 2: 0, 3: 0}
    for s in sends:
        if s["dst"] == me:
            due[s["step"]] += engines(s["mask"])
    mine = [s for s in sends if s["src"] == me]
    sent = sum(engines(s["mask"]) for s in mine)
    arr = {1: T.sem.a1, 2: T.sem.a2, 3: T.sem.a3}
    waited = []

    def need(step):
        if due[step] and step not in waited:
            g.wait_ge(arr[step], due[step])
            waited.append(step)

    g.sync.dma_start(T.xs[:], T.x[:]).then_inc(T.sem.ld, 16)
    g.wait_ge(T.sem.ld, 16)

    ncalls = 1 + max([s["call"] for s in mine])
    for call in range(ncalls):
        batch = [s for s in mine if s["call"] == call]
        step = batch[0]["step"]
        for earlier in range(1, step):
            need(earlier)
        transfers = []
        for s in batch:
            col, n, lo, dlo = s["col"], s["n"], s["lo"], s["dlo"]
            dst = T.cores[8 * s["dst"][0] + s["dst"][1]]
            assert s["mask"] & ~topo.mask(core, dst) == 0
            rid, pid = topo.addr(dst, core)
            srcs = [T.xs[:, col:col + n]]
            if step >= 2:
                srcs += [T.land1[:, i, lo:lo + n] for i in range(7)]
            if step == 3:
                srcs.append(T.land2[:, lo:lo + n])
            if s["where"] == "land1":
                out = T.land1[:, k if k < s["dst"][1] else k - 1, dlo:dlo + n]
            elif s["where"] == "pq":
                out = T["pq%d" % n][dlo]
            else:
                out = T[s["where"]][:, dlo:dlo + n]
            transfers.append(RemoteDMATransfer(dst_ids=[DstId(rid=rid, pnc=pid)], dma_engine_mask=s["mask"],
                                               remote_sem=arr[step], srcs=srcs, dsts=[out], alu_op=1 if step >= 2 else 0))
        g.remote_dma_fused(transfers, local_sem=T.sem.sent)

    for step in (1, 2, 3):
        need(step)
    w = W[rank]
    if w:
        if rank in whole:
            mine_half, other_half = T["pq%d" % w][0], T["pq%d" % w][1]
        else:
            mine_half, other_half = T.land3[:, 0:w], T.land3[:, w:2 * w]
        g.dma_start(mine_half, other_half, accum_op=AluOpType.add).then_inc(T.sem.loc, 16)
        g.wait_ge(T.sem.loc, 16)
        g.dma_start(T.y[:, 0:w], mine_half, allow_slow_non_contiguous=(w == 1)).then_inc(T.sem.loc, 16)
        g.wait_ge(T.sem.loc, 32)
    g.wait_ge(T.sem.sent, sent)
